import numpy as np
import ml_dtypes


def mxq(x, axis, fmt="e4m3"):
    dtype, down = {"e4m3": (ml_dtypes.float8_e4m3fn, 7), "e5m2": (ml_dtypes.float8_e5m2, 14)}[fmt]
    v = np.moveaxis(np.asarray(x, np.float32).astype(ml_dtypes.bfloat16).astype(np.float64), axis, -1)
    blocks = v.reshape(v.shape[:-1] + (-1, 32))
    amax = np.abs(blocks).max(-1, keepdims=True)
    byte = np.maximum(np.where(amax > 0, np.frexp(amax)[1] - 1 + 127, 0) - down, 1)
    scale = np.exp2(byte - 127.0)
    codes = (blocks / scale).astype(np.float32).astype(dtype).astype(np.float64)
    return np.moveaxis((codes * scale).reshape(v.shape), -1, axis)


WIDE = False


def mx_kscale(k):
    if not WIDE:
        return np.ones(k)
    levels = np.array([10, -10, 5, -5, 0])
    if k % 512:
        return np.exp2(np.random.permutation(np.resize(levels, k // 32))).repeat(32)
    a = np.empty((k // 512, 16))
    for p in range(k // 512):
        a[p, :8] = np.random.permutation(np.resize(levels, 8))
        for g in range(8):
            far = levels[np.abs(levels - a[p, g]) >= 10]
            a[p, g + 8] = far[np.random.randint(len(far))]
    return np.exp2(a.ravel()).repeat(32)


def f64(x):
    return np.asarray(x).astype(np.float64)


def striped(idx):
    return np.tile(idx.reshape(-1, 16).T, (8, 1)).astype(np.uint16)


def unstriped(offs):
    return offs[:16].T.reshape(-1).astype(np.int64)


def striped8(idx):
    return np.concatenate([x.reshape(-1, 16).T for x in idx]).astype(np.uint16)


def runs(offs, k):
    lists = np.stack([offs[16 * r : 16 * r + 16].T.reshape(-1) for r in range(8)]).astype(np.int64)
    return lists[np.arange(k) % 512 // 64]


def pack_weight(w):
    k, n = w.shape
    w = f64(np.asarray(w, np.float32).astype(ml_dtypes.bfloat16)).reshape(k // 32, 32, n)
    amax = np.abs(w).max(1)
    byte = np.clip(np.where(amax > 0, np.frexp(amax)[1] - 1 + 127 - 7, 1), 1, 254)
    scaled = (w * np.exp2(127.0 - byte)[:, None, :]).reshape(k, n).astype(np.float32)
    words = np.ascontiguousarray(scaled.reshape(k // 512, 128, 4, n).transpose(0, 1, 3, 2)).astype(ml_dtypes.float8_e4m3fn).view(np.uint8)
    return words, np.ascontiguousarray(byte.astype(np.uint8).reshape(k // 512, 16, n))


def unpack_weight(words, scales):
    g, p, n, _ = words.shape
    vals = np.ascontiguousarray(words).view(ml_dtypes.float8_e4m3fn).astype(np.float64) * np.repeat(np.exp2(scales.astype(np.float64) - 127.0), 8, axis=1)[..., None]
    return vals.transpose(0, 1, 3, 2).reshape(g * 512, n)


E2M1 = np.array([0.0, 0.5, 1.0, 1.5, 2.0, 3.0, 4.0, 6.0, -0.0, -0.5, -1.0, -1.5, -2.0, -3.0, -4.0, -6.0])


def pack_fp4(w):
    k, n = w.shape
    w = f64(np.asarray(w, np.float32).astype(ml_dtypes.bfloat16)).reshape(k // 32, 32, n)
    amax = np.abs(w).max(1)
    mant, ex = np.frexp(amax / 6.0)
    byte = np.clip(np.where(amax > 0, np.where(mant > 0.5, ex, ex - 1) + 127, 1), 1, 254)
    scaled = (w * np.exp2(127.0 - byte)[:, None, :]).reshape(k, n).astype(np.float32)
    c = np.ascontiguousarray(scaled.reshape(k // 512, 128, 4, n).transpose(0, 1, 3, 2)).astype(ml_dtypes.float4_e2m1fn).view(np.uint8) & 0xF
    words = (c[..., 0::2] | (c[..., 1::2] << 4)).reshape(k // 512, 128, 2 * n)
    return np.ascontiguousarray(words), np.ascontiguousarray(byte.astype(np.uint8).reshape(k // 512, 16, n))


def unpack_fp4(words, scales):
    g, _, n = scales.shape
    words = np.ascontiguousarray(words).reshape(g, 128, n, 2)
    nib = np.empty((g, 128, n, 4), np.uint8)
    nib[..., 0::2] = words & 0xF
    nib[..., 1::2] = words >> 4
    vals = E2M1[nib] * np.repeat(np.exp2(scales.astype(np.float64) - 127.0), 8, axis=1)[..., None]
    return vals.transpose(0, 1, 3, 2).reshape(g * 512, n)


def sigmoid(v):
    return 1.0 / (1.0 + np.exp(-np.maximum(v, -700.0)))

def planes(y):
    n, m = y.shape
    v = y.astype(np.float32).astype(ml_dtypes.bfloat16).astype(np.float64).reshape(n // 32, 32, m)
    top = np.abs(v).max(1)
    byte = np.clip(np.where(top > 0, np.frexp(top)[1] - 1 + 127 - 7, 1), 1, 254)
    codes = (v * np.exp2(127.0 - byte)[:, None, :]).reshape(n, m).astype(np.float32).astype(ml_dtypes.float8_e4m3fn).view(np.uint8)
    words = codes.reshape(n // 512, 128, 4, m).transpose(0, 1, 3, 2)
    return np.ascontiguousarray(words), np.ascontiguousarray(byte.astype(np.uint8).reshape(n // 512, 16, m))


K, T, S, N, H = 512, 2048, 512, 512, 512


def setup_inputs():
    n = np.random.standard_normal
    s = mx_kscale(K)[:, None]
    u = mx_kscale(S)
    packed_xT = pack_weight(n((K, T)) * s)
    packed_w1 = pack_fp4(n((S, N)) / np.sqrt(S) / u[:, None])
    return {
        "x_words": packed_xT[0],
        "x_scales": packed_xT[1],
        "wa": (n((K, H)) / np.sqrt(K) / s).astype(np.float32),
        "wb": (n((K, H)) / np.sqrt(K) / s).astype(np.float32),
        "gt": (np.random.uniform(0.5, 1.5, (S, 1)) * u[:, None]).astype(np.float32),
        "w1_words": packed_w1[0],
        "w1_scales": packed_w1[1],
        "offs": striped(np.random.permutation(T)[:S]),
        "two": striped(np.random.permutation(T)[:S]),
        "n1": striped8(np.stack([np.random.permutation(H) for _ in range(8)])),
        "n2": striped8(np.stack([np.random.permutation(H) for _ in range(8)])),
        "n3": striped8(np.stack([np.random.permutation(H) for _ in range(8)])),
    }


def reference(x_words, x_scales, wa, wb, gt, w1_words, w1_scales, offs, two, n1, n2, n3):
    xq = unpack_weight(x_words, x_scales)[:, unstriped(offs)]
    y = xq.T @ mxq(f64(wa), 0, "e4m3")
    x_two = unpack_weight(x_words, x_scales)[:, unstriped(two)]
    d = x_two.T @ mxq(f64(wb), 0, "e4m3")
    z = f64(gt) * (y * (sigmoid(d[np.arange(S)[:, None], runs(n2, S)])) - (0.5 * (y[np.arange(S)[:, None], runs(n1, S)])))
    h = unpack_fp4(w1_words, w1_scales).T @ mxq(z, 0, "e4m3")
    out_0 = h - (h[np.arange(N)[:, None], runs(n3, N)])
    return (out_0,) + planes(out_0)

@@ -1,0 +1,201 @@
+from contextlib import ExitStack
+
+import concourse.mybir as mybir
+
+F32 = mybir.dt.float32
+BF16 = mybir.dt.bfloat16
+I32 = mybir.dt.int32
+U32 = mybir.dt.uint32
+U16 = mybir.dt.uint16
+U8 = mybir.dt.uint8
+FP8X4 = mybir.dt.float8_e4m3fn_x4
+FP4X4 = mybir.dt.float4_e2m1fn_x4
+MULT = mybir.AluOpType.mult
+ADD = mybir.AluOpType.add
+ACT = mybir.ActivationFunctionType
+
+P = 128
+PACK = 4
+T = 2048
+W = 512
+HALF = W // 2
+FLOPS = 3 * 2 * W * W * W
+
+
+def tile_picked_twtgatebdif_none_po_kernel(
+    tc, x_words, x_scales, wa, wb, gt, w1_words, w1_scales, offs, two, n1, n2, n3, out_0, out_1, out_2
+):
+    nc = tc.nc
+    with ExitStack() as ctx:
+        sb = ctx.enter_context(tc.tile_pool(name="sb", bufs=1))
+        ps = ctx.enter_context(tc.psum_pool(name="ps", bufs=1))
+
+        def tile(name, shape, dtype):
+            return sb.tile(shape, dtype, name=name, align_bytes=64)
+
+        def load_list(name, src):
+            dst = sb.tile([P, W // 16], U16, name=name)
+            nc.sync.dma_start(dst[:], src)
+            return dst
+
+        def load_scale_rows(name, src, width, queue):
+            dst = tile(name, [P, width], U8)
+            nc.vector.memset(dst[:].bitcast(I32), 0)
+            for q in range(4):
+                queue.dma_start(dst[32 * q : 32 * q + 4, :].bitcast(I32), src[0, 4 * q : 4 * q + 4, :].bitcast(I32))
+            return dst
+
+        def cols(h):
+            return slice(h * HALF, (h + 1) * HALF)
+
+        def entries(lst, h):
+            return lst[:, h * HALF // 16 : (h + 1) * HALF // 16]
+
+        def interleave(engine_copy, dst, src):
+            engine_copy(
+                dst[:].rearrange("p (c i t) -> p c t i", i=4, t=PACK),
+                src[:].rearrange("p t (c i) -> p c t i", i=4),
+            )
+
+        two_t = load_list("two_t", two)
+        offs_t = load_list("offs_t", offs)
+        xs = load_scale_rows("xs", x_scales, T, nc.sync)
+        xw = tile("xw", [P, T], I32)
+        nc.sync.dma_start(xw[:], x_words[0].rearrange("p n t -> p (n t)").bitcast(I32))
+        raw = {}
+        for name, w in (("wb", wb), ("wa", wa)):
+            for h in range(2):
+                raw[name, h] = tile(f"{name}_raw{h}", [P, PACK, HALF], F32)
+                nc.sync.dma_start(raw[name, h][:], w.rearrange("(p j) c -> p j c", j=PACK)[:, :, cols(h)])
+        n2_t = load_list("n2_t", n2)
+        g = tile("g", [P, PACK], F32)
+        nc.sync.dma_start(g[:], gt.rearrange("(p t) o -> p (t o)", t=PACK))
+        n1_t = load_list("n1_t", n1)
+        w1w = tile("w1w", [P, 2 * W], U8)
+        nc.sync.dma_start(w1w[:].bitcast(I32), w1_words[0].bitcast(I32))
+        w1s = load_scale_rows("w1s", w1_scales, W, nc.sync)
+        n3_t = load_list("n3_t", n3)
+
+        def deal_bytes(name, src):
+            dst = tile(name, [P, W], U8)
+            nc.vector.tensor_copy(
+                dst[:].rearrange("p (t m) -> p t m", t=PACK), src[:].rearrange("p (m t) -> p t m", t=PACK)
+            )
+            return dst
+
+        def pick_scales(name, lst):
+            picked = tile(name + "_picked", [P, W], U8)
+            nc.vector.tensor_copy(picked[:], xs[:].indirect(lst[:]))
+            return deal_bytes(name, picked)
+
+        def pick_words(name, lst):
+            dst = tile(name, [P, W], U32)
+            nc.vector.tensor_copy(dst[:].rearrange("p (t m) -> p m t", t=PACK), xw[:].bitcast(U32).indirect(lst[:]))
+            return dst
+
+        def quantise_weight(name, copies):
+            codes = tile(name + "_codes", [P, W], U32)
+            scales = tile(name + "_scales", [P, W], U8)
+            for h in range(2):
+                rounded = tile(f"{name}_bf{h}", [P, HALF * PACK], BF16)
+                interleave(copies[h], rounded, raw[name, h])
+                nc.vector.quantize_mx(codes[:, cols(h)].bitcast(FP8X4), scales[:, cols(h)], rounded[:])
+            return codes, scales
+
+        def project(name, words, scales, w_codes, w_scales):
+            banks = []
+            for t in range(PACK):
+                bank = ps.tile([P, W], F32, name=f"{name}{t}", tag=f"{name}{t}")
+                rows = slice(t * P, (t + 1) * P)
+                nc.tensor.matmul_mx(
+                    bank[:],
+                    lhsT=words[:, rows].bitcast(FP8X4),
+                    lhsT_scale=scales[:, rows],
+                    rhs=w_codes[:].bitcast(FP8X4),
+                    rhs_scale=w_scales[:],
+                    start=True,
+                    stop=True,
+                )
+                banks.append(bank)
+            return banks
+
+        two_s = pick_scales("two_s", two_t)
+        offs_s = pick_scales("offs_s", offs_t)
+        two_w = pick_words("two_w", two_t)
+        wb_q = quantise_weight("wb", (nc.scalar.copy, nc.scalar.copy))
+        d_ps = project("bankd", two_w, two_s, *wb_q)
+        offs_w = pick_words("offs_w", offs_t)
+        wa_q = quantise_weight("wa", (nc.scalar.copy, nc.vector.tensor_copy))
+        y_ps = project("banky", offs_w, offs_s, *wa_q)
+
+        neg_half_g = tile("neg_half_g", [P, PACK], F32)
+        nc.vector.tensor_scalar(neg_half_g[:], g[:], -0.5, None, MULT)
+
+        w1_dealt = tile("w1_dealt", [P, 2 * W], U8)
+        nc.vector.tensor_copy(
+            w1_dealt[:].rearrange("p (t m b) -> p t m b", t=PACK, b=2),
+            w1w[:].rearrange("p (m t b) -> p t m b", t=PACK, b=2),
+        )
+        w1s_dealt = deal_bytes("w1s_dealt", w1s)
+
+        d_sb, u_sb, gate = [], [], {}
+        for t in range(PACK):
+            d_sb.append(tile(f"d_sb{t}", [P, W], F32))
+            nc.scalar.copy(d_sb[t][:], d_ps[t][:])
+            gate[t, 0] = tile(f"gate{t}_0", [P, HALF], F32)
+            nc.scalar.activation(gate[t, 0][:], d_sb[t][:].indirect(entries(n2_t, 0)), ACT.Sigmoid)
+            u_sb.append(tile(f"u_sb{t}", [P, W], F32))
+            nc.scalar.activation(u_sb[t][:], y_ps[t][:], ACT.Copy, scale=neg_half_g[:, t : t + 1])
+        for t in range(PACK):
+            gate[t, 1] = tile(f"gate{t}_1", [P, HALF], F32)
+            nc.scalar.activation(gate[t, 1][:], d_sb[t][:].indirect(entries(n2_t, 1)), ACT.Sigmoid)
+
+        neg_h = [tile(f"neg_h{t}", [P, W], F32) for t in range(PACK)]
+        pos_h = {}
+        for h in range(2):
+            z = tile(f"z{h}", [P, PACK, HALF], F32)
+            for t in range(PACK):
+                prod = tile(f"prod{t}_{h}", [P, HALF], F32)
+                nc.vector.scalar_tensor_tensor(prod[:], u_sb[t][:, cols(h)], -2.0, gate[t, h][:], MULT, MULT)
+                nc.vector.tensor_tensor(z[:, t, :], u_sb[t][:].indirect(entries(n1_t, h)), prod[:], ADD)
+            z_bf = tile(f"z_bf{h}", [P, HALF * PACK], BF16)
+            interleave(nc.vector.tensor_copy, z_bf, z)
+            z_codes = tile(f"z_codes{h}", [P, HALF], U32)
+            z_scales = tile(f"z_scales{h}", [P, HALF], U8)
+            nc.vector.quantize_mx(z_codes[:].bitcast(FP8X4), z_scales[:], z_bf[:])
+            h_ps = []
+            for t in range(PACK):
+                tag = ("bankd", "banky")[h] + str(t)
+                bank = ps.tile([P, W], F32, name=f"h{t}_{h}", tag=tag)
+                nc.tensor.matmul_mx(
+                    bank[:, :HALF],
+                    lhsT=w1_dealt[:, 2 * t * P : 2 * (t + 1) * P].bitcast(FP4X4),
+                    lhsT_scale=w1s_dealt[:, t * P : (t + 1) * P],
+                    rhs=z_codes[:].bitcast(FP8X4),
+                    rhs_scale=z_scales[:],
+                    start=True,
+                    stop=True,
+                )
+                nc.scalar.activation(neg_h[t][:, cols(h)], bank[:, :HALF], ACT.Copy, scale=-1.0)
+                h_ps.append(bank)
+            for t in range(PACK):
+                pos_h[t, h] = tile(f"pos_h{t}_{h}", [P, HALF], F32)
+                nc.scalar.copy(pos_h[t, h][:], h_ps[t][:, :HALF])
+
+        o_scales = tile("o_scales", [P, W], U8)
+        out_rows = out_0.rearrange("(p t) j -> p t j", t=PACK)
+        out_words = out_1[0].rearrange("p n t -> p (n t)").bitcast(I32)
+        for h in range(2):
+            o = tile(f"o{h}", [P, PACK, HALF], F32)
+            for t in range(PACK):
+                nc.vector.tensor_tensor(o[:, t, :], neg_h[t][:].indirect(entries(n3_t, h)), pos_h[t, h][:], ADD)
+                nc.sync.dma_start(out_rows[:, t, cols(h)], o[:, t, :])
+            o_bf = tile(f"o_bf{h}", [P, HALF * PACK], BF16)
+            interleave((nc.scalar.copy, nc.vector.tensor_copy)[h], o_bf, o)
+            o_codes = tile(f"o_codes{h}", [P, HALF], I32)
+            nc.vector.quantize_mx(o_codes[:].bitcast(FP8X4), o_scales[:, cols(h)], o_bf[:])
+            nc.sync.dma_start(out_words[:, cols(h)], o_codes[:])
+        for q in range(4):
+            (nc.sync, nc.scalar)[q % 2].dma_start(
+                out_2[0, 4 * q : 4 * q + 4, :].bitcast(I32), o_scales[32 * q : 32 * q + 4, :].bitcast(I32)
+            )

@@ -12,6 +12,7 @@ FP8X4 = mybir.dt.float8_e4m3fn_x4
 FP4X4 = mybir.dt.float4_e2m1fn_x4
 MULT = mybir.AluOpType.mult
 ADD = mybir.AluOpType.add
+SUB = mybir.AluOpType.subtract
 ACT = mybir.ActivationFunctionType
 
 P = 128
@@ -28,10 +29,11 @@ def tile_picked_twtgatebdif_none_po_kernel(
     nc = tc.nc
     with ExitStack() as ctx:
         sb = ctx.enter_context(tc.tile_pool(name="sb", bufs=1))
+        shared = ctx.enter_context(tc.tile_pool(name="shared", bufs=1))
         ps = ctx.enter_context(tc.psum_pool(name="ps", bufs=1))
 
-        def tile(name, shape, dtype):
-            return sb.tile(shape, dtype, name=name, align_bytes=64)
+        def tile(name, shape, dtype, tag=None):
+            return sb.tile(shape, dtype, name=name, tag=tag or name, align_bytes=64)
 
         def load_list(name, src):
             dst = sb.tile([P, W // 16], U16, name=name)
@@ -54,20 +56,34 @@ def tile_picked_twtgatebdif_none_po_kernel(
         def interleave(engine_copy, dst, src):
             engine_copy(
                 dst[:].rearrange("p (c i t) -> p c t i", i=4, t=PACK),
-                src[:].rearrange("p t (c i) -> p c t i", i=4),
+                src.rearrange("p t (c i) -> p c t i", i=4),
             )
 
+        def scalar_halve(dst, src):
+            nc.scalar.activation(dst, src, ACT.Copy, scale=-0.5)
+
+        def vector_halve(dst, src):
+            nc.vector.tensor_scalar(dst, src, -0.5, None, MULT)
+
+        raw = {}
+
+        def load_weight_half(name, w, h):
+            if name == "wa":
+                raw[name, h] = shared.tile([P, PACK, HALF], F32, name=f"wa_raw{h}", offset=h * PACK * HALF * 4)
+            else:
+                raw[name, h] = tile(f"{name}_raw{h}", [P, PACK, HALF], F32)
+            nc.sync.dma_start(raw[name, h][:], w.rearrange("(p j) c -> p j c", j=PACK)[:, :, cols(h)])
+
+        load_weight_half("wb", wb, 0)
+        load_weight_half("wb", wb, 1)
         two_t = load_list("two_t", two)
         offs_t = load_list("offs_t", offs)
         xs = load_scale_rows("xs", x_scales, T, nc.sync)
         xw = tile("xw", [P, T], I32)
         nc.sync.dma_start(xw[:], x_words[0].rearrange("p n t -> p (n t)").bitcast(I32))
-        raw = {}
-        for name, w in (("wb", wb), ("wa", wa)):
-            for h in range(2):
-                raw[name, h] = tile(f"{name}_raw{h}", [P, PACK, HALF], F32)
-                nc.sync.dma_start(raw[name, h][:], w.rearrange("(p j) c -> p j c", j=PACK)[:, :, cols(h)])
+        load_weight_half("wa", wa, 0)
         n2_t = load_list("n2_t", n2)
+        load_weight_half("wa", wa, 1)
         g = tile("g", [P, PACK], F32)
         nc.sync.dma_start(g[:], gt.rearrange("(p t) o -> p (t o)", t=PACK))
         n1_t = load_list("n1_t", n1)
@@ -75,30 +91,33 @@ def tile_picked_twtgatebdif_none_po_kernel(
         nc.sync.dma_start(w1w[:].bitcast(I32), w1_words[0].bitcast(I32))
         w1s = load_scale_rows("w1s", w1_scales, W, nc.sync)
         n3_t = load_list("n3_t", n3)
+        warm = tile("warm", [P, 2], F32)
+        nc.gpsimd.memset(warm[:, 0:1], 0.0)
+        nc.scalar.activation(warm[:, 1:2], warm[:, 0:1], ACT.Sigmoid)
 
-        def deal_bytes(name, src):
-            dst = tile(name, [P, W], U8)
+        def deal_bytes(name, src, tag=None):
+            dst = tile(name, [P, W], U8, tag)
             nc.vector.tensor_copy(
                 dst[:].rearrange("p (t m) -> p t m", t=PACK), src[:].rearrange("p (m t) -> p t m", t=PACK)
             )
             return dst
 
-        def pick_scales(name, lst):
-            picked = tile(name + "_picked", [P, W], U8)
+        def pick_scales(name, lst, tag=None):
+            picked = tile(name + "_picked", [P, W], U8, tag)
             nc.vector.tensor_copy(picked[:], xs[:].indirect(lst[:]))
             return deal_bytes(name, picked)
 
-        def pick_words(name, lst):
-            dst = tile(name, [P, W], U32)
+        def pick_words(name, lst, tag=None):
+            dst = tile(name, [P, W], U32, tag)
             nc.vector.tensor_copy(dst[:].rearrange("p (t m) -> p m t", t=PACK), xw[:].bitcast(U32).indirect(lst[:]))
             return dst
 
-        def quantise_weight(name, copies):
+        def quantise_weight(name, copies, tags):
             codes = tile(name + "_codes", [P, W], U32)
             scales = tile(name + "_scales", [P, W], U8)
             for h in range(2):
-                rounded = tile(f"{name}_bf{h}", [P, HALF * PACK], BF16)
-                interleave(copies[h], rounded, raw[name, h])
+                rounded = tile(f"{name}_bf{h}", [P, HALF * PACK], BF16, tags[h])
+                interleave(copies[h], rounded, raw[name, h][:])
                 nc.vector.quantize_mx(codes[:, cols(h)].bitcast(FP8X4), scales[:, cols(h)], rounded[:])
             return codes, scales
 
@@ -119,47 +138,46 @@ def tile_picked_twtgatebdif_none_po_kernel(
                 banks.append(bank)
             return banks
 
-        two_s = pick_scales("two_s", two_t)
-        offs_s = pick_scales("offs_s", offs_t)
-        two_w = pick_words("two_w", two_t)
-        wb_q = quantise_weight("wb", (nc.scalar.copy, nc.scalar.copy))
+        wb_q = quantise_weight("wb", (nc.vector.tensor_copy, nc.scalar.copy), ("wb_bf0", "wb_bf1"))
+        two_s = pick_scales("two_s", two_t, "wb_raw0")
+        offs_s = pick_scales("offs_s", offs_t, "wb_bf0")
+        two_w = pick_words("two_w", two_t, "wb_raw1")
         d_ps = project("bankd", two_w, two_s, *wb_q)
-        offs_w = pick_words("offs_w", offs_t)
-        wa_q = quantise_weight("wa", (nc.scalar.copy, nc.vector.tensor_copy))
+        offs_w = pick_words("offs_w", offs_t, "wb_bf1")
+        wa_q = quantise_weight("wa", (nc.scalar.copy, nc.vector.tensor_copy), ("wa_bf0", "xw"))
         y_ps = project("banky", offs_w, offs_s, *wa_q)
 
-        neg_half_g = tile("neg_half_g", [P, PACK], F32)
-        nc.vector.tensor_scalar(neg_half_g[:], g[:], -0.5, None, MULT)
-
-        w1_dealt = tile("w1_dealt", [P, 2 * W], U8)
-        nc.vector.tensor_copy(
-            w1_dealt[:].rearrange("p (t m b) -> p t m b", t=PACK, b=2),
-            w1w[:].rearrange("p (m t b) -> p t m b", t=PACK, b=2),
-        )
-        w1s_dealt = deal_bytes("w1s_dealt", w1s)
 
         d_sb, u_sb, gate = [], [], {}
-        for t in range(PACK):
-            d_sb.append(tile(f"d_sb{t}", [P, W], F32))
-            nc.scalar.copy(d_sb[t][:], d_ps[t][:])
-            gate[t, 0] = tile(f"gate{t}_0", [P, HALF], F32)
-            nc.scalar.activation(gate[t, 0][:], d_sb[t][:].indirect(entries(n2_t, 0)), ACT.Sigmoid)
-            u_sb.append(tile(f"u_sb{t}", [P, W], F32))
-            nc.scalar.activation(u_sb[t][:], y_ps[t][:], ACT.Copy, scale=neg_half_g[:, t : t + 1])
-        for t in range(PACK):
-            gate[t, 1] = tile(f"gate{t}_1", [P, HALF], F32)
-            nc.scalar.activation(gate[t, 1][:], d_sb[t][:].indirect(entries(n2_t, 1)), ACT.Sigmoid)
 
         neg_h = [tile(f"neg_h{t}", [P, W], F32) for t in range(PACK)]
         pos_h = {}
         for h in range(2):
             z = tile(f"z{h}", [P, PACK, HALF], F32)
             for t in range(PACK):
-                prod = tile(f"prod{t}_{h}", [P, HALF], F32)
-                nc.vector.scalar_tensor_tensor(prod[:], u_sb[t][:, cols(h)], -2.0, gate[t, h][:], MULT, MULT)
-                nc.vector.tensor_tensor(z[:, t, :], u_sb[t][:].indirect(entries(n1_t, h)), prod[:], ADD)
+                if h == 0:
+                    d_sb.append(shared.tile([P, W], F32, name=f"d_sb{t}", offset=t * W * 4))
+                    nc.scalar.copy(d_sb[t][:], d_ps[t][:])
+                gate[t, h] = sb.tile([P, HALF], F32, name=f"gate{t}_{h}", tag="gate", bufs=3)
+                nc.scalar.activation(gate[t, h][:], d_sb[t][:].indirect(entries(n2_t, h)), ACT.Sigmoid)
+                if h == 0:
+                    u_sb.append(tile(f"u_sb{t}", [P, W], F32))
+                    if t == 0:
+                        nc.vector.tensor_scalar(u_sb[t][:], y_ps[t][:], g[:, t : t + 1], None, MULT)
+                    else:
+                        nc.scalar.activation(u_sb[t][:], y_ps[t][:], ACT.Copy, scale=g[:, t : t + 1])
+                prod = sb.tile([P, HALF], F32, name=f"prod{t}_{h}", tag="prod", bufs=2)
+                nc.vector.scalar_tensor_tensor(prod[:], u_sb[t][:, cols(h)], 2.0, gate[t, h][:], MULT, MULT)
+                nc.vector.tensor_tensor(z[:, t, :], u_sb[t][:].indirect(entries(n1_t, h)), prod[:], SUB)
             z_bf = tile(f"z_bf{h}", [P, HALF * PACK], BF16)
-            interleave(nc.vector.tensor_copy, z_bf, z)
+            interleave((scalar_halve, vector_halve)[h], z_bf, z[:])
+            if h == 0:
+                w1_dealt = tile("w1_dealt", [P, 2 * W], U8, "xw")
+                nc.vector.tensor_copy(
+                    w1_dealt[:].rearrange("p (t m b) -> p t m b", t=PACK, b=2),
+                    w1w[:].rearrange("p (m t b) -> p t m b", t=PACK, b=2),
+                )
+                w1s_dealt = deal_bytes("w1s_dealt", w1s, "offs_s")
             z_codes = tile(f"z_codes{h}", [P, HALF], U32)
             z_scales = tile(f"z_scales{h}", [P, HALF], U8)
             nc.vector.quantize_mx(z_codes[:].bitcast(FP8X4), z_scales[:], z_bf[:])
@@ -191,11 +209,11 @@ def tile_picked_twtgatebdif_none_po_kernel(
                 nc.vector.tensor_tensor(o[:, t, :], neg_h[t][:].indirect(entries(n3_t, h)), pos_h[t, h][:], ADD)
                 nc.sync.dma_start(out_rows[:, t, cols(h)], o[:, t, :])
             o_bf = tile(f"o_bf{h}", [P, HALF * PACK], BF16)
-            interleave((nc.scalar.copy, nc.vector.tensor_copy)[h], o_bf, o)
+            interleave((nc.scalar.copy, nc.vector.tensor_copy)[h], o_bf, o[:])
             o_codes = tile(f"o_codes{h}", [P, HALF], I32)
             nc.vector.quantize_mx(o_codes[:].bitcast(FP8X4), o_scales[:, cols(h)], o_bf[:])
-            nc.sync.dma_start(out_words[:, cols(h)], o_codes[:])
+            nc.scalar.dma_start(out_words[:, cols(h)], o_codes[:])
         for q in range(4):
-            (nc.sync, nc.scalar)[q % 2].dma_start(
+            (nc.sync, nc.sync, nc.scalar, nc.sync)[q].dma_start(
                 out_2[0, 4 * q : 4 * q + 4, :].bitcast(I32), o_scales[32 * q : 32 * q + 4, :].bitcast(I32)
             )

@@ -17,9 +17,21 @@ ACT = mybir.ActivationFunctionType
 
 P = 128
 PACK = 4
-T = 2048
+TOKENS = 2048
 W = 512
 HALF = W // 2
+GROUP = 16
+QUADRANTS = 4
+RUN = 4
+
+WA_HALF_BYTES = PACK * HALF * 4
+D_TILE_BYTES = W * 4
+X_WORDS_AT = 2 * WA_HALF_BYTES
+DEALT_SCALES_AT = X_WORDS_AT + PACK * HALF * 2
+
+GATES_AHEAD = 3
+PRODUCTS_AHEAD = 2
+
 FLOPS = 3 * 2 * W * W * W
 
 
@@ -32,93 +44,78 @@ def tile_picked_twtgatebdif_none_po_kernel(
         shared = ctx.enter_context(tc.tile_pool(name="shared", bufs=1))
         ps = ctx.enter_context(tc.psum_pool(name="ps", bufs=1))
 
-        def tile(name, shape, dtype, tag=None):
-            return sb.tile(shape, dtype, name=name, tag=tag or name, align_bytes=64)
+        def tile(name, shape, dtype, after=None):
+            return sb.tile(shape, dtype, name=name, tag=after or name, align_bytes=64)
+
+        def placed(name, shape, dtype, offset):
+            return shared.tile(shape, dtype, name=name, offset=offset, align_bytes=64)
+
+        def cols(half):
+            return slice(half * HALF, (half + 1) * HALF)
+
+        def spans(pieces):
+            width = HALF // pieces
+            return [slice(k * width, (k + 1) * width) for k in range(pieces)]
+
+        def entries(lst, half, span):
+            first = half * HALF
+            return lst[:, (first + span.start) // GROUP : (first + span.stop) // GROUP]
 
         def load_list(name, src):
-            dst = sb.tile([P, W // 16], U16, name=name)
+            dst = sb.tile([P, W // GROUP], U16, name=name)
             nc.sync.dma_start(dst[:], src)
             return dst
 
-        def load_scale_rows(name, src, width, queue):
+        def load_scale_rows(name, src, width, queues):
             dst = tile(name, [P, width], U8)
             nc.vector.memset(dst[:].bitcast(I32), 0)
-            for q in range(4):
-                queue.dma_start(dst[32 * q : 32 * q + 4, :].bitcast(I32), src[0, 4 * q : 4 * q + 4, :].bitcast(I32))
+            for q in range(QUADRANTS):
+                queues[q].dma_start(dst[32 * q : 32 * q + 4, :].bitcast(I32), src[0, 4 * q : 4 * q + 4, :].bitcast(I32))
             return dst
 
-        def cols(h):
-            return slice(h * HALF, (h + 1) * HALF)
+        def load_weight_half(dst, w, half):
+            nc.sync.dma_start(dst[:], w.rearrange("(p t) c -> p t c", t=PACK)[:, :, cols(half)])
+            return dst
 
-        def entries(lst, h):
-            return lst[:, h * HALF // 16 : (h + 1) * HALF // 16]
+        def round_and_quantise(copy, pieces, src, rounded, codes, scales):
+            for c in spans(pieces):
+                copy(
+                    rounded[:, c.start * PACK : c.stop * PACK].rearrange("p (c i t) -> p c t i", i=RUN, t=PACK),
+                    src[:, :, c].rearrange("p t (c i) -> p c t i", i=RUN),
+                )
+            for c in spans(pieces):
+                nc.vector.quantize_mx(codes[:, c].bitcast(FP8X4), scales[:, c], rounded[:, c.start * PACK : c.stop * PACK])
 
-        def interleave(engine_copy, dst, src):
-            engine_copy(
-                dst[:].rearrange("p (c i t) -> p c t i", i=4, t=PACK),
-                src.rearrange("p t (c i) -> p c t i", i=4),
-            )
+        def gather_with(dst, source, lst, half, t, other, op):
+            last = half == 1 and t == PACK - 1
+            for c in spans(2 if last else 1):
+                nc.vector.tensor_tensor(dst[:, c], source[:].indirect(entries(lst, half, c)), other[:, c], op)
 
-        def scalar_halve(dst, src):
-            nc.scalar.activation(dst, src, ACT.Copy, scale=-0.5)
-
-        def vector_halve(dst, src):
-            nc.vector.tensor_scalar(dst, src, -0.5, None, MULT)
-
-        raw = {}
-
-        def load_weight_half(name, w, h):
-            if name == "wa":
-                raw[name, h] = shared.tile([P, PACK, HALF], F32, name=f"wa_raw{h}", offset=h * PACK * HALF * 4)
-            else:
-                raw[name, h] = tile(f"{name}_raw{h}", [P, PACK, HALF], F32)
-            nc.sync.dma_start(raw[name, h][:], w.rearrange("(p j) c -> p j c", j=PACK)[:, :, cols(h)])
-
-        load_weight_half("wb", wb, 0)
-        load_weight_half("wb", wb, 1)
-        two_t = load_list("two_t", two)
-        offs_t = load_list("offs_t", offs)
-        xs = load_scale_rows("xs", x_scales, T, nc.sync)
-        xw = tile("xw", [P, T], I32)
-        nc.sync.dma_start(xw[:], x_words[0].rearrange("p n t -> p (n t)").bitcast(I32))
-        load_weight_half("wa", wa, 0)
-        n2_t = load_list("n2_t", n2)
-        load_weight_half("wa", wa, 1)
-        g = tile("g", [P, PACK], F32)
-        nc.sync.dma_start(g[:], gt.rearrange("(p t) o -> p (t o)", t=PACK))
-        n1_t = load_list("n1_t", n1)
-        w1w = tile("w1w", [P, 2 * W], U8)
-        nc.sync.dma_start(w1w[:].bitcast(I32), w1_words[0].bitcast(I32))
-        w1s = load_scale_rows("w1s", w1_scales, W, nc.sync)
-        n3_t = load_list("n3_t", n3)
-        warm = tile("warm", [P, 2], F32)
-        nc.gpsimd.memset(warm[:, 0:1], 0.0)
-        nc.scalar.activation(warm[:, 1:2], warm[:, 0:1], ACT.Sigmoid)
-
-        def deal_bytes(name, src, tag=None):
-            dst = tile(name, [P, W], U8, tag)
+        def deal_bytes(dst, src):
             nc.vector.tensor_copy(
                 dst[:].rearrange("p (t m) -> p t m", t=PACK), src[:].rearrange("p (m t) -> p t m", t=PACK)
             )
             return dst
 
-        def pick_scales(name, lst, tag=None):
-            picked = tile(name + "_picked", [P, W], U8, tag)
-            nc.vector.tensor_copy(picked[:], xs[:].indirect(lst[:]))
-            return deal_bytes(name, picked)
-
-        def pick_words(name, lst, tag=None):
-            dst = tile(name, [P, W], U32, tag)
-            nc.vector.tensor_copy(dst[:].rearrange("p (t m) -> p m t", t=PACK), xw[:].bitcast(U32).indirect(lst[:]))
+        def pick_scales(name, lst, after):
+            dst = tile(name, [P, W], U8, after)
+            nc.vector.tensor_copy(dst[:], x_scale_rows[:].indirect(lst[:]))
             return dst
 
-        def quantise_weight(name, copies, tags):
+        def pick_words(name, lst, after):
+            dst = tile(name, [P, W], U32, after)
+            nc.vector.tensor_copy(
+                dst[:].rearrange("p (t m) -> p m t", t=PACK), x_word_rows[:].bitcast(U32).indirect(lst[:])
+            )
+            return dst
+
+        def quantise_weight(name, raw, rounded, copies, pieces):
             codes = tile(name + "_codes", [P, W], U32)
             scales = tile(name + "_scales", [P, W], U8)
-            for h in range(2):
-                rounded = tile(f"{name}_bf{h}", [P, HALF * PACK], BF16, tags[h])
-                interleave(copies[h], rounded, raw[name, h][:])
-                nc.vector.quantize_mx(codes[:, cols(h)].bitcast(FP8X4), scales[:, cols(h)], rounded[:])
+            for half in range(2):
+                round_and_quantise(
+                    copies[half], pieces[half], raw[half], rounded[half], codes[:, cols(half)], scales[:, cols(half)]
+                )
             return codes, scales
 
         def project(name, words, scales, w_codes, w_scales):
@@ -138,82 +135,115 @@ def tile_picked_twtgatebdif_none_po_kernel(
                 banks.append(bank)
             return banks
 
-        wb_q = quantise_weight("wb", (nc.vector.tensor_copy, nc.scalar.copy), ("wb_bf0", "wb_bf1"))
-        two_s = pick_scales("two_s", two_t, "wb_raw0")
-        offs_s = pick_scales("offs_s", offs_t, "wb_bf0")
-        two_w = pick_words("two_w", two_t, "wb_raw1")
-        d_ps = project("bankd", two_w, two_s, *wb_q)
-        offs_w = pick_words("offs_w", offs_t, "wb_bf1")
-        wa_q = quantise_weight("wa", (nc.scalar.copy, nc.vector.tensor_copy), ("wa_bf0", "xw"))
-        y_ps = project("banky", offs_w, offs_s, *wa_q)
+        def scale_on_scalar(factor):
+            return lambda dst, src: nc.scalar.activation(dst, src, ACT.Copy, scale=factor)
 
+        def scale_on_vector(factor):
+            return lambda dst, src: nc.vector.tensor_scalar(dst, src, factor, None, MULT)
 
-        d_sb, u_sb, gate = [], [], {}
+        wb_raw = [tile(f"wb_raw{half}", [P, PACK, HALF], F32) for half in range(2)]
+        wa_raw = [placed(f"wa_raw{half}", [P, PACK, HALF], F32, half * WA_HALF_BYTES) for half in range(2)]
+        load_weight_half(wb_raw[0], wb, 0)
+        two_list = load_list("two_list", two)
+        offs_list = load_list("offs_list", offs)
+        x_scale_rows = load_scale_rows("x_scale_rows", x_scales, TOKENS, (nc.scalar, nc.scalar, nc.sync, nc.sync))
+        warm = tile("warm", [P, 2], F32)
+        nc.vector.memset(warm[:, 0:1], 0.0)
+        nc.scalar.activation(warm[:, 1:2], warm[:, 0:1], ACT.Sigmoid)
+        load_weight_half(wb_raw[1], wb, 1)
+        x_word_rows = placed("x_word_rows", [P, TOKENS], I32, X_WORDS_AT)
+        nc.sync.dma_start(x_word_rows[:], x_words[0].rearrange("p n t -> p (n t)").bitcast(I32))
+        load_weight_half(wa_raw[0], wa, 0)
+        n2_list = load_list("n2_list", n2)
+        load_weight_half(wa_raw[1], wa, 1)
+        gain = tile("gain", [P, PACK], F32)
+        nc.sync.dma_start(gain[:], gt.rearrange("(p t) o -> p (t o)", t=PACK))
+        n1_list = load_list("n1_list", n1)
+        w1_word_rows = tile("w1_word_rows", [P, 2 * W], U8)
+        nc.sync.dma_start(w1_word_rows[:].bitcast(I32), w1_words[0].bitcast(I32))
+        w1_scale_rows = load_scale_rows("w1_scale_rows", w1_scales, W, (nc.sync,) * QUADRANTS)
+        n3_list = load_list("n3_list", n3)
 
+        wb_rounded = [tile(f"wb_rounded{half}", [P, HALF * PACK], BF16) for half in range(2)]
+        wb_codes, wb_scales = quantise_weight("wb", wb_raw, wb_rounded, (nc.vector.tensor_copy, nc.scalar.copy), (1, 1))
+        two_picked = pick_scales("two_picked", two_list, "wb_raw0")
+        offs_picked = pick_scales("offs_picked", offs_list, "wb_rounded0")
+        two_scales = deal_bytes(tile("two_scales", [P, W], U8), two_picked)
+        two_words = pick_words("two_words", two_list, "wb_raw1")
+        d_banks = project("d_bank", two_words, two_scales, wb_codes, wb_scales)
+        offs_words = pick_words("offs_words", offs_list, "wb_rounded1")
+        offs_scales = deal_bytes(placed("offs_scales", [P, W], U8, DEALT_SCALES_AT), offs_picked)
+        wa_rounded = [
+            tile("wa_rounded0", [P, HALF * PACK], BF16),
+            placed("wa_rounded1", [P, HALF * PACK], BF16, X_WORDS_AT),
+        ]
+        wa_codes, wa_scales = quantise_weight("wa", wa_raw, wa_rounded, (nc.scalar.copy, nc.vector.tensor_copy), (1, 2))
+        y_banks = project("y_bank", offs_words, offs_scales, wa_codes, wa_scales)
+
+        d_rows, gy_rows = [], []
         neg_h = [tile(f"neg_h{t}", [P, W], F32) for t in range(PACK)]
-        pos_h = {}
-        for h in range(2):
-            z = tile(f"z{h}", [P, PACK, HALF], F32)
+        h_half = {}
+        for half in range(2):
+            neg_2z = tile(f"neg_2z{half}", [P, PACK, HALF], F32)
             for t in range(PACK):
-                if h == 0:
-                    d_sb.append(shared.tile([P, W], F32, name=f"d_sb{t}", offset=t * W * 4))
-                    nc.scalar.copy(d_sb[t][:], d_ps[t][:])
-                gate[t, h] = sb.tile([P, HALF], F32, name=f"gate{t}_{h}", tag="gate", bufs=3)
-                nc.scalar.activation(gate[t, h][:], d_sb[t][:].indirect(entries(n2_t, h)), ACT.Sigmoid)
-                if h == 0:
-                    u_sb.append(tile(f"u_sb{t}", [P, W], F32))
-                    if t == 0:
-                        nc.vector.tensor_scalar(u_sb[t][:], y_ps[t][:], g[:, t : t + 1], None, MULT)
-                    else:
-                        nc.scalar.activation(u_sb[t][:], y_ps[t][:], ACT.Copy, scale=g[:, t : t + 1])
-                prod = sb.tile([P, HALF], F32, name=f"prod{t}_{h}", tag="prod", bufs=2)
-                nc.vector.scalar_tensor_tensor(prod[:], u_sb[t][:, cols(h)], 2.0, gate[t, h][:], MULT, MULT)
-                nc.vector.tensor_tensor(z[:, t, :], u_sb[t][:].indirect(entries(n1_t, h)), prod[:], SUB)
-            z_bf = tile(f"z_bf{h}", [P, HALF * PACK], BF16)
-            interleave((scalar_halve, vector_halve)[h], z_bf, z[:])
-            if h == 0:
-                w1_dealt = tile("w1_dealt", [P, 2 * W], U8, "xw")
+                if half == 0:
+                    d_rows.append(placed(f"d_rows{t}", [P, W], F32, t * D_TILE_BYTES))
+                    nc.scalar.copy(d_rows[t][:], d_banks[t][:])
+                gate = sb.tile([P, HALF], F32, name=f"gate{t}_{half}", tag="gate", bufs=GATES_AHEAD)
+                nc.scalar.activation(gate[:], d_rows[t][:].indirect(entries(n2_list, half, slice(0, HALF))), ACT.Sigmoid)
+                if half == 0:
+                    scale_by = scale_on_vector if t == 0 else scale_on_scalar
+                    gy_rows.append(tile(f"gy_rows{t}", [P, W], F32))
+                    scale_by(gain[:, t : t + 1])(gy_rows[t][:], y_banks[t][:])
+                product = sb.tile([P, HALF], F32, name=f"product{t}_{half}", tag="product", bufs=PRODUCTS_AHEAD)
+                nc.vector.scalar_tensor_tensor(product[:], gy_rows[t][:, cols(half)], 2.0, gate[:], MULT, MULT)
+                gather_with(neg_2z[:, t, :], gy_rows[t], n1_list, half, t, product, SUB)
+            z_rounded = tile(f"z_rounded{half}", [P, HALF * PACK], BF16)
+            if half == 0:
+                w1_dealt = placed("w1_dealt", [P, 2 * W], U8, X_WORDS_AT)
                 nc.vector.tensor_copy(
                     w1_dealt[:].rearrange("p (t m b) -> p t m b", t=PACK, b=2),
-                    w1w[:].rearrange("p (m t b) -> p t m b", t=PACK, b=2),
+                    w1_word_rows[:].rearrange("p (m t b) -> p t m b", t=PACK, b=2),
                 )
-                w1s_dealt = deal_bytes("w1s_dealt", w1s, "offs_s")
-            z_codes = tile(f"z_codes{h}", [P, HALF], U32)
-            z_scales = tile(f"z_scales{h}", [P, HALF], U8)
-            nc.vector.quantize_mx(z_codes[:].bitcast(FP8X4), z_scales[:], z_bf[:])
-            h_ps = []
+                w1_dealt_scales = deal_bytes(placed("w1_dealt_scales", [P, W], U8, DEALT_SCALES_AT), w1_scale_rows)
+            z_codes = tile(f"z_codes{half}", [P, HALF], U32)
+            z_scales = tile(f"z_scales{half}", [P, HALF], U8)
+            rounding = (scale_on_scalar, scale_on_vector)[half](-0.5)
+            round_and_quantise(rounding, half + 1, neg_2z, z_rounded, z_codes, z_scales)
+            h_banks = []
             for t in range(PACK):
-                tag = ("bankd", "banky")[h] + str(t)
-                bank = ps.tile([P, W], F32, name=f"h{t}_{h}", tag=tag)
+                bank = ps.tile([P, W], F32, name=f"h_bank{t}_{half}", tag=("d_bank", "y_bank")[half] + str(t))
                 nc.tensor.matmul_mx(
                     bank[:, :HALF],
                     lhsT=w1_dealt[:, 2 * t * P : 2 * (t + 1) * P].bitcast(FP4X4),
-                    lhsT_scale=w1s_dealt[:, t * P : (t + 1) * P],
+                    lhsT_scale=w1_dealt_scales[:, t * P : (t + 1) * P],
                     rhs=z_codes[:].bitcast(FP8X4),
                     rhs_scale=z_scales[:],
                     start=True,
                     stop=True,
                 )
-                nc.scalar.activation(neg_h[t][:, cols(h)], bank[:, :HALF], ACT.Copy, scale=-1.0)
-                h_ps.append(bank)
+                scale_by = scale_on_vector if half == 1 and t == 0 else scale_on_scalar
+                scale_by(-1.0)(neg_h[t][:, cols(half)], bank[:, :HALF])
+                h_banks.append(bank)
             for t in range(PACK):
-                pos_h[t, h] = tile(f"pos_h{t}_{h}", [P, HALF], F32)
-                nc.scalar.copy(pos_h[t, h][:], h_ps[t][:, :HALF])
+                h_half[t, half] = tile(f"h_half{t}_{half}", [P, HALF], F32)
+                nc.scalar.copy(h_half[t, half][:], h_banks[t][:, :HALF])
 
-        o_scales = tile("o_scales", [P, W], U8)
+        out_scales = tile("out_scales", [P, W], U8)
         out_rows = out_0.rearrange("(p t) j -> p t j", t=PACK)
         out_words = out_1[0].rearrange("p n t -> p (n t)").bitcast(I32)
-        for h in range(2):
-            o = tile(f"o{h}", [P, PACK, HALF], F32)
+        for half in range(2):
+            result = tile(f"result{half}", [P, PACK, HALF], F32)
+            tiles_a_store = PACK // (half + 1)
             for t in range(PACK):
-                nc.vector.tensor_tensor(o[:, t, :], neg_h[t][:].indirect(entries(n3_t, h)), pos_h[t, h][:], ADD)
-                nc.sync.dma_start(out_rows[:, t, cols(h)], o[:, t, :])
-            o_bf = tile(f"o_bf{h}", [P, HALF * PACK], BF16)
-            interleave((nc.scalar.copy, nc.vector.tensor_copy)[h], o_bf, o[:])
-            o_codes = tile(f"o_codes{h}", [P, HALF], I32)
-            nc.vector.quantize_mx(o_codes[:].bitcast(FP8X4), o_scales[:, cols(h)], o_bf[:])
-            nc.scalar.dma_start(out_words[:, cols(h)], o_codes[:])
-        for q in range(4):
-            (nc.sync, nc.sync, nc.scalar, nc.sync)[q].dma_start(
-                out_2[0, 4 * q : 4 * q + 4, :].bitcast(I32), o_scales[32 * q : 32 * q + 4, :].bitcast(I32)
-            )
+                gather_with(result[:, t, :], neg_h[t], n3_list, half, t, h_half[t, half], ADD)
+                if (t + 1) % tiles_a_store == 0:
+                    done = slice(t + 1 - tiles_a_store, t + 1)
+                    nc.sync.dma_start(out_rows[:, done, cols(half)], result[:, done, :])
+            out_rounded = tile(f"out_rounded{half}", [P, HALF * PACK], BF16)
+            out_codes = tile(f"out_codes{half}", [P, HALF], I32)
+            rounding = (nc.scalar.copy, nc.vector.tensor_copy)[half]
+            round_and_quantise(rounding, half + 1, result, out_rounded, out_codes, out_scales[:, cols(half)])
+            nc.scalar.dma_start(out_words[:, cols(half)], out_codes[:])
+        for q, queue in enumerate((nc.sync, nc.sync, nc.scalar, nc.sync)):
+            queue.dma_start(out_2[0, 4 * q : 4 * q + 4, :].bitcast(I32), out_scales[32 * q : 32 * q + 4, :].bitcast(I32))

from contextlib import ExitStack

import concourse.mybir as mybir

F32 = mybir.dt.float32
BF16 = mybir.dt.bfloat16
I32 = mybir.dt.int32
U32 = mybir.dt.uint32
U16 = mybir.dt.uint16
U8 = mybir.dt.uint8
FP8X4 = mybir.dt.float8_e4m3fn_x4
FP4X4 = mybir.dt.float4_e2m1fn_x4
MULT = mybir.AluOpType.mult
ADD = mybir.AluOpType.add
SUB = mybir.AluOpType.subtract
ACT = mybir.ActivationFunctionType

P = 128
PACK = 4
TOKENS = 2048
W = 512
HALF = W // 2
GROUP = 16
QUADRANTS = 4
RUN = 4

WA_HALF_BYTES = PACK * HALF * 4
D_TILE_BYTES = W * 4
X_WORDS_AT = 2 * WA_HALF_BYTES
DEALT_SCALES_AT = X_WORDS_AT + PACK * HALF * 2

GATES_AHEAD = 3
PRODUCTS_AHEAD = 2

FLOPS = 3 * 2 * W * W * W


def tile_picked_twtgatebdif_none_po_kernel(
    tc, x_words, x_scales, wa, wb, gt, w1_words, w1_scales, offs, two, n1, n2, n3, out_0, out_1, out_2
):
    nc = tc.nc
    with ExitStack() as ctx:
        sb = ctx.enter_context(tc.tile_pool(name="sb", bufs=1))
        shared = ctx.enter_context(tc.tile_pool(name="shared", bufs=1))
        ps = ctx.enter_context(tc.psum_pool(name="ps", bufs=1))

        def tile(name, shape, dtype, after=None):
            return sb.tile(shape, dtype, name=name, tag=after or name, align_bytes=64)

        def placed(name, shape, dtype, offset):
            return shared.tile(shape, dtype, name=name, offset=offset, align_bytes=64)

        def cols(half):
            return slice(half * HALF, (half + 1) * HALF)

        def spans(pieces):
            width = HALF // pieces
            return [slice(k * width, (k + 1) * width) for k in range(pieces)]

        def entries(lst, half, span):
            first = half * HALF
            return lst[:, (first + span.start) // GROUP : (first + span.stop) // GROUP]

        def load_list(name, src):
            dst = sb.tile([P, W // GROUP], U16, name=name)
            nc.sync.dma_start(dst[:], src)
            return dst

        def load_scale_rows(name, src, width, queues):
            dst = tile(name, [P, width], U8)
            nc.vector.memset(dst[:].bitcast(I32), 0)
            for q in range(QUADRANTS):
                queues[q].dma_start(dst[32 * q : 32 * q + 4, :].bitcast(I32), src[0, 4 * q : 4 * q + 4, :].bitcast(I32))
            return dst

        def load_weight_half(dst, w, half):
            nc.sync.dma_start(dst[:], w.rearrange("(p t) c -> p t c", t=PACK)[:, :, cols(half)])
            return dst

        def round_and_quantise(copy, pieces, src, rounded, codes, scales):
            for c in spans(pieces):
                copy(
                    rounded[:, c.start * PACK : c.stop * PACK].rearrange("p (c i t) -> p c t i", i=RUN, t=PACK),
                    src[:, :, c].rearrange("p t (c i) -> p c t i", i=RUN),
                )
            for c in spans(pieces):
                nc.vector.quantize_mx(codes[:, c].bitcast(FP8X4), scales[:, c], rounded[:, c.start * PACK : c.stop * PACK])

        def gather_with(dst, source, lst, half, t, other, op):
            last = half == 1 and t == PACK - 1
            for c in spans(2 if last else 1):
                nc.vector.tensor_tensor(dst[:, c], source[:].indirect(entries(lst, half, c)), other[:, c], op)

        def deal_bytes(dst, src):
            nc.vector.tensor_copy(
                dst[:].rearrange("p (t m) -> p t m", t=PACK), src[:].rearrange("p (m t) -> p t m", t=PACK)
            )
            return dst

        def pick_scales(name, lst, after):
            dst = tile(name, [P, W], U8, after)
            nc.vector.tensor_copy(dst[:], x_scale_rows[:].indirect(lst[:]))
            return dst

        def pick_words(name, lst, after):
            dst = tile(name, [P, W], U32, after)
            nc.vector.tensor_copy(
                dst[:].rearrange("p (t m) -> p m t", t=PACK), x_word_rows[:].bitcast(U32).indirect(lst[:])
            )
            return dst

        def quantise_weight(name, raw, rounded, copies, pieces):
            codes = tile(name + "_codes", [P, W], U32)
            scales = tile(name + "_scales", [P, W], U8)
            for half in range(2):
                round_and_quantise(
                    copies[half], pieces[half], raw[half], rounded[half], codes[:, cols(half)], scales[:, cols(half)]
                )
            return codes, scales

        def project(name, words, scales, w_codes, w_scales):
            banks = []
            for t in range(PACK):
                bank = ps.tile([P, W], F32, name=f"{name}{t}", tag=f"{name}{t}")
                rows = slice(t * P, (t + 1) * P)
                nc.tensor.matmul_mx(
                    bank[:],
                    lhsT=words[:, rows].bitcast(FP8X4),
                    lhsT_scale=scales[:, rows],
                    rhs=w_codes[:].bitcast(FP8X4),
                    rhs_scale=w_scales[:],
                    start=True,
                    stop=True,
                )
                banks.append(bank)
            return banks

        def scale_on_scalar(factor):
            return lambda dst, src: nc.scalar.activation(dst, src, ACT.Copy, scale=factor)

        def scale_on_vector(factor):
            return lambda dst, src: nc.vector.tensor_scalar(dst, src, factor, None, MULT)

        wb_raw = [tile(f"wb_raw{half}", [P, PACK, HALF], F32) for half in range(2)]
        wa_raw = [placed(f"wa_raw{half}", [P, PACK, HALF], F32, half * WA_HALF_BYTES) for half in range(2)]
        load_weight_half(wb_raw[0], wb, 0)
        two_list = load_list("two_list", two)
        offs_list = load_list("offs_list", offs)
        x_scale_rows = load_scale_rows("x_scale_rows", x_scales, TOKENS, (nc.scalar, nc.scalar, nc.sync, nc.sync))
        warm = tile("warm", [P, 2], F32)
        nc.vector.memset(warm[:, 0:1], 0.0)
        nc.scalar.activation(warm[:, 1:2], warm[:, 0:1], ACT.Sigmoid)
        load_weight_half(wb_raw[1], wb, 1)
        x_word_rows = placed("x_word_rows", [P, TOKENS], I32, X_WORDS_AT)
        nc.sync.dma_start(x_word_rows[:], x_words[0].rearrange("p n t -> p (n t)").bitcast(I32))
        load_weight_half(wa_raw[0], wa, 0)
        n2_list = load_list("n2_list", n2)
        load_weight_half(wa_raw[1], wa, 1)
        gain = tile("gain", [P, PACK], F32)
        nc.sync.dma_start(gain[:], gt.rearrange("(p t) o -> p (t o)", t=PACK))
        n1_list = load_list("n1_list", n1)
        w1_word_rows = tile("w1_word_rows", [P, 2 * W], U8)
        nc.sync.dma_start(w1_word_rows[:].bitcast(I32), w1_words[0].bitcast(I32))
        w1_scale_rows = load_scale_rows("w1_scale_rows", w1_scales, W, (nc.sync,) * QUADRANTS)
        n3_list = load_list("n3_list", n3)

        wb_rounded = [tile(f"wb_rounded{half}", [P, HALF * PACK], BF16) for half in range(2)]
        wb_codes, wb_scales = quantise_weight("wb", wb_raw, wb_rounded, (nc.vector.tensor_copy, nc.scalar.copy), (1, 1))
        two_picked = pick_scales("two_picked", two_list, "wb_raw0")
        offs_picked = pick_scales("offs_picked", offs_list, "wb_rounded0")
        two_scales = deal_bytes(tile("two_scales", [P, W], U8), two_picked)
        two_words = pick_words("two_words", two_list, "wb_raw1")
        d_banks = project("d_bank", two_words, two_scales, wb_codes, wb_scales)
        offs_words = pick_words("offs_words", offs_list, "wb_rounded1")
        offs_scales = deal_bytes(placed("offs_scales", [P, W], U8, DEALT_SCALES_AT), offs_picked)
        wa_rounded = [
            tile("wa_rounded0", [P, HALF * PACK], BF16),
            placed("wa_rounded1", [P, HALF * PACK], BF16, X_WORDS_AT),
        ]
        wa_codes, wa_scales = quantise_weight("wa", wa_raw, wa_rounded, (nc.scalar.copy, nc.vector.tensor_copy), (1, 2))
        y_banks = project("y_bank", offs_words, offs_scales, wa_codes, wa_scales)

        d_rows, gy_rows = [], []
        neg_h = [tile(f"neg_h{t}", [P, W], F32) for t in range(PACK)]
        h_half = {}
        for half in range(2):
            neg_2z = tile(f"neg_2z{half}", [P, PACK, HALF], F32)
            for t in range(PACK):
                if half == 0:
                    d_rows.append(placed(f"d_rows{t}", [P, W], F32, t * D_TILE_BYTES))
                    nc.scalar.copy(d_rows[t][:], d_banks[t][:])
                gate = sb.tile([P, HALF], F32, name=f"gate{t}_{half}", tag="gate", bufs=GATES_AHEAD)
                nc.scalar.activation(gate[:], d_rows[t][:].indirect(entries(n2_list, half, slice(0, HALF))), ACT.Sigmoid)
                if half == 0:
                    scale_by = scale_on_vector if t == 0 else scale_on_scalar
                    gy_rows.append(tile(f"gy_rows{t}", [P, W], F32))
                    scale_by(gain[:, t : t + 1])(gy_rows[t][:], y_banks[t][:])
                product = sb.tile([P, HALF], F32, name=f"product{t}_{half}", tag="product", bufs=PRODUCTS_AHEAD)
                nc.vector.scalar_tensor_tensor(product[:], gy_rows[t][:, cols(half)], 2.0, gate[:], MULT, MULT)
                gather_with(neg_2z[:, t, :], gy_rows[t], n1_list, half, t, product, SUB)
            z_rounded = tile(f"z_rounded{half}", [P, HALF * PACK], BF16)
            if half == 0:
                w1_dealt = placed("w1_dealt", [P, 2 * W], U8, X_WORDS_AT)
                nc.vector.tensor_copy(
                    w1_dealt[:].rearrange("p (t m b) -> p t m b", t=PACK, b=2),
                    w1_word_rows[:].rearrange("p (m t b) -> p t m b", t=PACK, b=2),
                )
                w1_dealt_scales = deal_bytes(placed("w1_dealt_scales", [P, W], U8, DEALT_SCALES_AT), w1_scale_rows)
            z_codes = tile(f"z_codes{half}", [P, HALF], U32)
            z_scales = tile(f"z_scales{half}", [P, HALF], U8)
            rounding = (scale_on_scalar, scale_on_vector)[half](-0.5)
            round_and_quantise(rounding, half + 1, neg_2z, z_rounded, z_codes, z_scales)
            h_banks = []
            for t in range(PACK):
                bank = ps.tile([P, W], F32, name=f"h_bank{t}_{half}", tag=("d_bank", "y_bank")[half] + str(t))
                nc.tensor.matmul_mx(
                    bank[:, :HALF],
                    lhsT=w1_dealt[:, 2 * t * P : 2 * (t + 1) * P].bitcast(FP4X4),
                    lhsT_scale=w1_dealt_scales[:, t * P : (t + 1) * P],
                    rhs=z_codes[:].bitcast(FP8X4),
                    rhs_scale=z_scales[:],
                    start=True,
                    stop=True,
                )
                scale_by = scale_on_vector if half == 1 and t == 0 else scale_on_scalar
                scale_by(-1.0)(neg_h[t][:, cols(half)], bank[:, :HALF])
                h_banks.append(bank)
            for t in range(PACK):
                h_half[t, half] = tile(f"h_half{t}_{half}", [P, HALF], F32)
                nc.scalar.copy(h_half[t, half][:], h_banks[t][:, :HALF])

        out_scales = tile("out_scales", [P, W], U8)
        out_rows = out_0.rearrange("(p t) j -> p t j", t=PACK)
        out_words = out_1[0].rearrange("p n t -> p (n t)").bitcast(I32)
        for half in range(2):
            result = tile(f"result{half}", [P, PACK, HALF], F32)
            tiles_a_store = PACK // (half + 1)
            for t in range(PACK):
                gather_with(result[:, t, :], neg_h[t], n3_list, half, t, h_half[t, half], ADD)
                if (t + 1) % tiles_a_store == 0:
                    done = slice(t + 1 - tiles_a_store, t + 1)
                    nc.sync.dma_start(out_rows[:, done, cols(half)], result[:, done, :])
            out_rounded = tile(f"out_rounded{half}", [P, HALF * PACK], BF16)
            out_codes = tile(f"out_codes{half}", [P, HALF], I32)
            rounding = (nc.scalar.copy, nc.vector.tensor_copy)[half]
            round_and_quantise(rounding, half + 1, result, out_rounded, out_codes, out_scales[:, cols(half)])
            nc.scalar.dma_start(out_words[:, cols(half)], out_codes[:])
        for q, queue in enumerate((nc.sync, nc.sync, nc.scalar, nc.sync)):
            queue.dma_start(out_2[0, 4 * q : 4 * q + 4, :].bitcast(I32), out_scales[32 * q : 32 * q + 4, :].bitcast(I32))
